import numpy as np, ml_dtypes
CORES = [2,10,50,58,66,74,122]
N = 7
import mx_ref
NC, G = 128, 2
C = np.float32(0.00869)
BF = ml_dtypes.bfloat16
def cut(t, i, w=512):
    return t[:, w * i:w * i + w]
def tile(rs):
    return np.stack(rs, axis=2).reshape(128, -1).astype(BF)
def layer(w, X):
    out = []
    for i in range(G):
        for t in range(len(X)):
            p = mx_ref.matmul(mx_ref.quantize(cut(w, len(X) * i + t)), X[t])
            z = p if t == 0 else z + p
        out.append(z)
    return out
def act(Z):
    return [np.maximum(s * z, 0) * C for z in Z for s in (1, -1)]
def setup_inputs(rng):
    def f(*shape):
        return mx_ref.flush((rng.standard_normal(shape, dtype=np.float32) * np.exp2(rng.integers(-2, 3, shape[:-1] + (1,)))).astype(BF))
    return {"x": f(N, 128, 4 * NC), "w1": f(N, 128, G * N * 512), "w2": f(N, 128, 2 * 512)}
def setup_inputs_blocks(rng):
    d = setup_inputs(rng)
    for k in ("x", "w1", "w2"): d[k] = mx_ref.spread(d[k], rng, 4)
    return d
def setup_inputs_wide(rng):
    d = setup_inputs(rng)
    for k in ("x", "w1", "w2"): d[k] = mx_ref.flush((d[k].astype(np.float32) * np.exp2(rng.integers(-6, 7, (N, 1, 1))).astype(np.float32)).astype(BF))
    return d
def reference(x, w1, w2, own=None):
    X = [mx_ref.quantize(x[j]) for j in range(N)]
    h = np.stack([tile(act(layer(w1[r], X))) for r in range(N)])
    use = h if own is None else own["h"]
    H = [mx_ref.quantize(use[j]) for j in range(N)]
    y = np.zeros((N, 128, NC), np.float32)
    for r in range(N):
        y[r] = mx_ref.matmul(mx_ref.quantize(cut(w2[r], 0)), H[r]) + mx_ref.matmul(mx_ref.quantize(cut(w2[r], 1)), H[(r + 1) % N])
    return {"h": h, "y": y}

@@ -1,0 +1,168 @@
+from concourse.bass import DstId, RemoteDMATransfer
+from concourse.mybir import dt, ActivationFunctionType
+
+N = 7
+NC = 128
+TW = 512
+C = 0.00869
+PRE = 4
+FIRST = {1: [1], 2: [2], 3: [3], 4: [4], 5: [5], 6: [4, 2]}
+LAST = {1: [1], 2: [1, 1], 3: [2, 1], 4: [3, 1], 5: [4, 1], 6: [4, 2], 7: [4, 2, 1]}
+MAXCH = 5
+
+SCRATCH = {
+    "xt": ("sbuf", [128, TW], "bfloat16"),
+    "w1t": ("sbuf", [128, 2 * N * TW], "bfloat16"),
+    "w2t": ("sbuf", [128, 2 * TW], "bfloat16"),
+    "ht": ("sbuf", [128, TW], "bfloat16"),
+    "yt": ("sbuf", [128, NC], "float32"),
+    "xc": ("sbuf", [128, N * NC], "float8_e4m3fn_x4"),
+    "xs": ("sbuf", [128, N * NC], "uint8"),
+    "w1c": ("sbuf", [128, 2 * N * NC], "float8_e4m3fn_x4"),
+    "w1s": ("sbuf", [128, 2 * N * NC], "uint8"),
+    "w2c": ("sbuf", [128, 2 * NC], "float8_e4m3fn_x4"),
+    "w2s": ("sbuf", [128, 2 * NC], "uint8"),
+    "hc": ("sbuf", [128, 2 * NC], "float8_e4m3fn_x4"),
+    "hs": ("sbuf", [128, 2 * NC], "uint8"),
+    "zp": ("psum", [128, 3 * 512], "float32"),
+}
+SEMAPHORES = (["lx", "lsec", "xq", "xsent", "gate", "z0", "z1", "rdone", "hq", "hsent", "hgate", "w2q", "harr", "ymm",
+               "ycp", "yst", "hst", "pin", "cin", "fsent"]
+              + ["lw%d" % i for i in range(MAXCH)] + ["wq%d" % k for k in range(2 * N)] + ["arr%d" % j for j in range(N)])
+
+
+def _count(mask):
+    return bin(mask).count("1")
+
+
+def _helpers(rc, T, topo):
+    others = [d for d in T.cores if d != rc]
+    cand = [c for c in range(topo.CORES_PER_CHIP * topo.CHIPS)
+            if topo.chip(c) == topo.chip(rc) and c not in T.cores and all(topo.may_write(c, d) for d in others)]
+    return sorted(cand, key=lambda c: (topo.die(c) != topo.die(rc), c))[:3]
+
+
+def _multi(src_core, dsts, topo, src, dst, sem):
+    mask = topo.mask(src_core, dsts[0])
+    for d in dsts:
+        mask &= topo.mask(src_core, d)
+    ids = [DstId(rid=topo.addr(d)[0], pnc=topo.addr(d)[1]) for d in dsts]
+    return RemoteDMATransfer(dst_ids=ids, dma_engine_mask=mask, remote_sem=sem, srcs=[src], dsts=[dst for _ in dsts]), _count(mask)
+
+
+def _pieces(r):
+    out = [(0, PRE), (PRE, N)]
+    runs = [(N, 2 * N)] if r == 0 else [(N + r, 2 * N), (N, N + r)]
+    for i, (a, b) in enumerate(runs):
+        for n in (LAST if i == len(runs) - 1 else FIRST)[b - a]:
+            out.append((a, a + n))
+            a += n
+    return out
+
+
+def _helper_program(g, core, T, topo, s, h):
+    sl = slice(NC * s, NC * s + NC)
+    early, late = T.cores[(s - (h + 1)) % N], T.cores[(s - (h + 4)) % N]
+    n_in = _count(topo.mask(T.cores[s], core))
+    arr = T.sem["arr%d" % s]
+    sent = 0
+    g.wait_ge(T.sem.pin, n_in)
+    t, n = _multi(core, [early, late], topo, T.xs[:, sl], T.xs[:, sl], arr)
+    g.remote_dma_fused([t], local_sem=T.sem.fsent)
+    sent += n
+    g.wait_ge(T.sem.cin, n_in)
+    for d in (early, late):
+        rid, pid, _ = topo.addr(d)
+        m = topo.mask(core, d)
+        g.remote_dma(T.xc[:, sl].bitcast(dt.uint8), T.xc[:, sl].bitcast(dt.uint8), arr, T.sem.fsent, pid, rid, m)
+        sent += _count(m)
+    g.wait_ge(T.sem.fsent, sent)
+
+
+def rank_program(g, core, T, topo):
+    r = T.rank_of(core)
+    if r is None:
+        for s, rc in enumerate(T.cores):
+            hs = _helpers(rc, T, topo)
+            if core in hs:
+                _helper_program(g, core, T, topo, s, hs.index(core))
+        return
+
+    S = T.sem
+    own = slice(NC * r, NC * r + NC)
+    pieces = _pieces(r)
+
+    g.sync.dma_start(T.xt[:], T.x[:]).then_inc(S.lx, 16)
+    for i, (a, b) in enumerate(pieces):
+        if i == 1:
+            g.sync.wait_ge(S.gate, 1)
+        g.sync.dma_start(T.w1t[:, TW * a:TW * b], T.w1[:, TW * a:TW * b]).then_inc(S["lw%d" % i], 16)
+    g.sync.dma_start(T.w2t[:], T.w2[:]).then_inc(S.lsec, 16)
+    g.sync.wait_ge(S.ycp, 1)
+    g.sync.dma_start(T.y[:], T.yt[:]).then_inc(S.yst, 16)
+    g.sync.wait_ge(S.yst, 16)
+
+    g.vector.wait_ge(S.lx, 16)
+    g.vector.quantize_mx(T.xc[:, own], T.xs[:, own], T.xt[:]).then_inc(S.xq, 1)
+    for i, (a, b) in enumerate(pieces):
+        g.vector.wait_ge(S["lw%d" % i], 16)
+        for k in range(a, b):
+            g.vector.quantize_mx(T.w1c[:, NC * k:NC * k + NC], T.w1s[:, NC * k:NC * k + NC],
+                                 T.w1t[:, TW * k:TW * k + TW]).then_inc(S["wq%d" % k], 1)
+    g.vector.wait_ge(S.rdone, 4)
+    g.vector.quantize_mx(T.hc[:, 0:NC], T.hs[:, 0:NC], T.ht[:]).then_inc(S.hq, 1)
+    g.vector.wait_ge(S.lsec, 16)
+    g.vector.quantize_mx(T.w2c[:], T.w2s[:], T.w2t[:]).then_inc(S.w2q, 1)
+    g.vector.wait_ge(S.ymm, 1)
+    g.vector.tensor_copy(T.yt[:], T.zp[:, 1024:1024 + NC]).then_inc(S.ycp, 1)
+
+    helpers = _helpers(core, T, topo)
+    g.wait_ge(S.xq, 1)
+    tp, n_on = _multi(core, helpers, topo, T.xs[:, own], T.xs[:, own], S.pin)
+    g.remote_dma_fused([tp], local_sem=S.xsent)
+    tc, _ = _multi(core, helpers, topo, T.xc[:, own].bitcast(dt.uint8), T.xc[:, own].bitcast(dt.uint8), S.cin)
+    g.remote_dma_fused([tc], local_sem=S.xsent)
+    g.sem_inc(S.gate, 1)
+    prev = T.cores[(r - 1) % N]
+    rid, pid, _ = topo.addr(prev)
+    hm = topo.mask(core, prev)
+    g.wait_ge(S.hq, 1)
+    g.remote_dma(T.hc[:, NC:2 * NC].bitcast(dt.uint8), T.hc[:, 0:NC].bitcast(dt.uint8), S.harr, S.hsent, pid, rid, hm)
+    g.remote_dma(T.hs[:, NC:2 * NC], T.hs[:, 0:NC], S.harr, S.hsent, pid, rid, hm)
+    g.sem_inc(S.hgate, 1)
+    g.wait_ge(S.xsent, 2 * n_on)
+    g.wait_ge(S.hsent, 2 * _count(hm))
+
+    groups = [[r], [(r + o) % N for o in (1, 2, 3)], [(r + o) % N for o in (4, 5, 6)]]
+    seq = [(i, j) for grp in groups for i in (0, 1) for j in grp]
+    done = [0, 0]
+    for i, j in seq:
+        k = N * i + j
+        if j == r:
+            g.tensor.wait_ge(S.xq, 1)
+        else:
+            src = _helpers(T.cores[j], T, topo)[((j - r) % N - 1) % 3]
+            g.tensor.wait_ge(S["arr%d" % j], 2 * _count(topo.mask(src, core)))
+        g.tensor.wait_ge(S["wq%d" % k], 1)
+        done[i] += 1
+        mm = g.tensor.matmul_mx(T.zp[:, 512 * i:512 * i + NC], T.w1c[:, NC * k:NC * k + NC], T.w1s[:, NC * k:NC * k + NC],
+                                T.xc[:, NC * j:NC * j + NC], T.xs[:, NC * j:NC * j + NC], done[i] == 1, done[i] == N)
+        if done[i] == N:
+            mm.then_inc(S["z%d" % i], 1)
+    g.tensor.wait_ge(S.hq, 1)
+    g.tensor.wait_ge(S.w2q, 1)
+    g.tensor.matmul_mx(T.zp[:, 1024:1024 + NC], T.w2c[:, 0:NC], T.w2s[:, 0:NC], T.hc[:, 0:NC], T.hs[:, 0:NC], True, False)
+    nxt = T.cores[(r + 1) % N]
+    g.tensor.wait_ge(S.harr, 2 * _count(topo.mask(nxt, core)))
+    g.tensor.matmul_mx(T.zp[:, 1024:1024 + NC], T.w2c[:, NC:2 * NC], T.w2s[:, NC:2 * NC], T.hc[:, NC:2 * NC],
+                       T.hs[:, NC:2 * NC], False, True).then_inc(S.ymm, 1)
+
+    for i in (0, 1):
+        g.scalar.wait_ge(S["z%d" % i], 1)
+        for b, sc in ((2 * i, C), (2 * i + 1, -C)):
+            g.scalar.activation(T.ht[:, b:TW:4], T.zp[:, 512 * i:512 * i + NC], ActivationFunctionType.Relu,
+                                scale=sc).then_inc(S.rdone, 1)
+    g.scalar.wait_ge(S.rdone, 4)
+    g.scalar.wait_ge(S.hgate, 1)
+    g.scalar.dma_start(T.h[:], T.ht[:]).then_inc(S.hst, 16)
+    g.scalar.wait_ge(S.hst, 16)

@@ -1,5 +1,5 @@
 from concourse.bass import DstId, RemoteDMATransfer
-from concourse.mybir import dt, ActivationFunctionType
+from concourse.mybir import dt, AluOpType, ActivationFunctionType
 
 N = 7
 NC = 128
@@ -30,6 +30,9 @@ SEMAPHORES = (["lx", "lsec", "xq", "xsent", "gate", "z0", "z1", "rdone", "hq", "
                "ycp", "yst", "hst", "pin", "cin", "fsent"]
               + ["lw%d" % i for i in range(MAXCH)] + ["wq%d" % k for k in range(2 * N)] + ["arr%d" % j for j in range(N)])
 
+KINDS = [(True, 0), (False, 0), (True, 1), (False, 1), (True, 2), (False, 2)]
+_CACHE = {}
+
 
 def _count(mask):
     return bin(mask).count("1")
@@ -39,7 +42,99 @@ def _helpers(rc, T, topo):
     others = [d for d in T.cores if d != rc]
     cand = [c for c in range(topo.CORES_PER_CHIP * topo.CHIPS)
             if topo.chip(c) == topo.chip(rc) and c not in T.cores and all(topo.may_write(c, d) for d in others)]
-    return sorted(cand, key=lambda c: (topo.die(c) != topo.die(rc), c))[:3]
+    near = [c for c in cand if topo.die(c) == topo.die(rc)]
+    far = [c for c in cand if topo.die(c) != topo.die(rc)]
+    return near[0], far[0], far[1]
+
+
+def _route(a, b, topo):
+    if a == b:
+        return []
+    if topo.same_plane(a, b):
+        return [("out", a), ("in", b)]
+    if topo.mates(a, b):
+        return [("mate", a)]
+    m = [c for c in range(topo.CHIPS) if topo.mates(a, c)][0]
+    return [("mate", a), ("out", m), ("in", b)]
+
+
+def _subsets(items, k):
+    if k == 0:
+        return [[]]
+    return [[items[i]] + rest for i in range(len(items)) for rest in _subsets(items[i + 1:], k - 1)]
+
+
+def _match(edges, n):
+    owner = {}
+
+    def aug(s, seen):
+        for d in range(n):
+            if (s, d) in edges and d not in seen:
+                seen.add(d)
+                if d not in owner or aug(owner[d], seen):
+                    owner[d] = s
+                    return True
+        return False
+
+    for s in range(n):
+        aug(s, set())
+    return {s: d for d, s in owner.items()}
+
+
+def _plan(T, topo):
+    if "plan" in _CACHE:
+        return _CACHE["plan"]
+    n = len(T.cores)
+    ch = [topo.chip(c) for c in T.cores]
+    total = {}
+    for s in range(n):
+        for d in range(n):
+            for l in _route(ch[s], ch[d], topo):
+                total[l] = total.get(l, 0) + 1
+    half = (n - 1) // 2
+    res = []
+
+    def rec(s, load, got):
+        if s == n:
+            return True
+        others = [d for d in range(n) if d != s]
+        for near in _subsets(others, half):
+            l2, g2, ok = dict(load), dict(got), True
+            for d in others:
+                side = d in near
+                g2[(d, side)] = g2.get((d, side), 0) + 1
+                ok = ok and g2[(d, side)] <= half
+                for l in _route(ch[s], ch[d], topo):
+                    l2[(l, side)] = l2.get((l, side), 0) + 1
+                    ok = ok and l2[(l, side)] <= (total[l] + 1) // 2
+            if ok:
+                res.append(near)
+                if rec(s + 1, l2, g2):
+                    return True
+                res.pop()
+        return False
+
+    rec(0, {}, {})
+    kind = {}
+    for side in (True, False):
+        edges = {(s, d) for s in range(n) for d in range(n) if d != s and (d in res[s]) == side}
+        for k in range(half):
+            for s, d in _match(edges, n).items():
+                kind[(s, d)] = (side, k)
+                edges.discard((s, d))
+    _CACHE["plan"] = kind
+    return kind
+
+
+def _dest(kind, s, k):
+    return [d for d in range(N) if kind.get((s, d)) == k][0]
+
+
+def _sender(T, topo, s, k):
+    near, far2, far1 = _helpers(T.cores[s], T, topo)
+    if k[0]:
+        return T.cores[s] if k[1] == 0 else near
+    return far1 if k[1] == 0 else far2
 
 
 def _multi(src_core, dsts, topo, src, dst, sem):
@@ -60,32 +155,37 @@ def _pieces(r):
     return out
 
 
-def _helper_program(g, core, T, topo, s, h):
+def _pass_on(g, core, T, topo, s, dsts, sem_sent):
     sl = slice(NC * s, NC * s + NC)
-    early, late = T.cores[(s - (h + 1)) % N], T.cores[(s - (h + 4)) % N]
-    n_in = _count(topo.mask(T.cores[s], core))
-    arr = T.sem["arr%d" % s]
     sent = 0
-    g.wait_ge(T.sem.pin, n_in)
-    t, n = _multi(core, [early, late], topo, T.xs[:, sl], T.xs[:, sl], arr)
-    g.remote_dma_fused([t], local_sem=T.sem.fsent)
-    sent += n
-    g.wait_ge(T.sem.cin, n_in)
-    for d in (early, late):
+    for d in dsts:
         rid, pid, _ = topo.addr(d)
         m = topo.mask(core, d)
-        g.remote_dma(T.xc[:, sl].bitcast(dt.uint8), T.xc[:, sl].bitcast(dt.uint8), arr, T.sem.fsent, pid, rid, m)
+        g.remote_dma(T.xc[:, sl].bitcast(dt.uint8), T.xc[:, sl].bitcast(dt.uint8), T.sem["arr%d" % s], sem_sent, pid, rid, m)
         sent += _count(m)
+    return sent
+
+
+def _helper_program(g, core, T, topo, s, dsts):
+    sl = slice(NC * s, NC * s + NC)
+    n_in = _count(topo.mask(T.cores[s], core))
+    g.wait_ge(T.sem.pin, n_in)
+    t, sent = _multi(core, dsts, topo, T.xs[:, sl], T.xs[:, sl], T.sem["arr%d" % s])
+    g.remote_dma_fused([t], local_sem=T.sem.fsent)
+    g.wait_ge(T.sem.cin, n_in)
+    sent += _pass_on(g, core, T, topo, s, dsts, T.sem.fsent)
     g.wait_ge(T.sem.fsent, sent)
 
 
 def rank_program(g, core, T, topo):
     r = T.rank_of(core)
+    kind = _plan(T, topo)
     if r is None:
         for s, rc in enumerate(T.cores):
-            hs = _helpers(rc, T, topo)
-            if core in hs:
-                _helper_program(g, core, T, topo, s, hs.index(core))
+            near, far2, far1 = _helpers(rc, T, topo)
+            for h, ks in ((near, [(True, 1), (True, 2)]), (far2, [(False, 1), (False, 2)]), (far1, [(False, 0)])):
+                if core == h:
+                    _helper_program(g, core, T, topo, s, [T.cores[_dest(kind, s, k)] for k in ks])
         return
 
     S = T.sem
@@ -96,8 +196,8 @@ def rank_program(g, core, T, topo):
     for i, (a, b) in enumerate(pieces):
         if i == 1:
             g.sync.wait_ge(S.gate, 1)
+            g.sync.dma_start(T.w2t[:], T.w2[:]).then_inc(S.lsec, 16)
         g.sync.dma_start(T.w1t[:, TW * a:TW * b], T.w1[:, TW * a:TW * b]).then_inc(S["lw%d" % i], 16)
-    g.sync.dma_start(T.w2t[:], T.w2[:]).then_inc(S.lsec, 16)
     g.sync.wait_ge(S.ycp, 1)
     g.sync.dma_start(T.y[:], T.yt[:]).then_inc(S.yst, 16)
     g.sync.wait_ge(S.yst, 16)
@@ -105,23 +205,32 @@ def rank_program(g, core, T, topo):
     g.vector.wait_ge(S.lx, 16)
     g.vector.quantize_mx(T.xc[:, own], T.xs[:, own], T.xt[:]).then_inc(S.xq, 1)
     for i, (a, b) in enumerate(pieces):
+        if i == 1:
+            g.vector.wait_ge(S.lsec, 16)
+            g.vector.quantize_mx(T.w2c[:], T.w2s[:], T.w2t[:]).then_inc(S.w2q, 1)
         g.vector.wait_ge(S["lw%d" % i], 16)
         for k in range(a, b):
             g.vector.quantize_mx(T.w1c[:, NC * k:NC * k + NC], T.w1s[:, NC * k:NC * k + NC],
                                  T.w1t[:, TW * k:TW * k + TW]).then_inc(S["wq%d" % k], 1)
+    g.vector.wait_ge(S.z1, 1)
+    for b, sc in ((2, C), (3, -C)):
+        g.vector.tensor_scalar(T.ht[:, b:TW:4], T.zp[:, 512:512 + NC], sc, 0.0, AluOpType.mult,
+                               AluOpType.max).then_inc(S.rdone, 1)
     g.vector.wait_ge(S.rdone, 4)
     g.vector.quantize_mx(T.hc[:, 0:NC], T.hs[:, 0:NC], T.ht[:]).then_inc(S.hq, 1)
-    g.vector.wait_ge(S.lsec, 16)
-    g.vector.quantize_mx(T.w2c[:], T.w2s[:], T.w2t[:]).then_inc(S.w2q, 1)
     g.vector.wait_ge(S.ymm, 1)
     g.vector.tensor_copy(T.yt[:], T.zp[:, 1024:1024 + NC]).then_inc(S.ycp, 1)
 
-    helpers = _helpers(core, T, topo)
+    helpers = list(_helpers(core, T, topo))
     g.wait_ge(S.xq, 1)
     tp, n_on = _multi(core, helpers, topo, T.xs[:, own], T.xs[:, own], S.pin)
     g.remote_dma_fused([tp], local_sem=S.xsent)
     tc, _ = _multi(core, helpers, topo, T.xc[:, own].bitcast(dt.uint8), T.xc[:, own].bitcast(dt.uint8), S.cin)
     g.remote_dma_fused([tc], local_sem=S.xsent)
+    straight = [T.cores[_dest(kind, r, (True, 0))]]
+    td, n_off = _multi(core, straight, topo, T.xs[:, own], T.xs[:, own], S["arr%d" % r])
+    g.remote_dma_fused([td], local_sem=S.xsent)
+    n_off += _pass_on(g, core, T, topo, r, straight, S.xsent)
     g.sem_inc(S.gate, 1)
     prev = T.cores[(r - 1) % N]
     rid, pid, _ = topo.addr(prev)
@@ -130,25 +239,23 @@ def rank_program(g, core, T, topo):
     g.remote_dma(T.hc[:, NC:2 * NC].bitcast(dt.uint8), T.hc[:, 0:NC].bitcast(dt.uint8), S.harr, S.hsent, pid, rid, hm)
     g.remote_dma(T.hs[:, NC:2 * NC], T.hs[:, 0:NC], S.harr, S.hsent, pid, rid, hm)
     g.sem_inc(S.hgate, 1)
-    g.wait_ge(S.xsent, 2 * n_on)
+    g.wait_ge(S.xsent, 2 * n_on + n_off)
     g.wait_ge(S.hsent, 2 * _count(hm))
 
-    groups = [[r], [(r + o) % N for o in (1, 2, 3)], [(r + o) % N for o in (4, 5, 6)]]
-    seq = [(i, j) for grp in groups for i in (0, 1) for j in grp]
-    done = [0, 0]
-    for i, j in seq:
-        k = N * i + j
+    order = [r] + sorted([j for j in range(N) if j != r], key=lambda j: KINDS.index(kind[(j, r)]))
+    for n_done, j in enumerate(order):
         if j == r:
             g.tensor.wait_ge(S.xq, 1)
         else:
-            src = _helpers(T.cores[j], T, topo)[((j - r) % N - 1) % 3]
-            g.tensor.wait_ge(S["arr%d" % j], 2 * _count(topo.mask(src, core)))
-        g.tensor.wait_ge(S["wq%d" % k], 1)
-        done[i] += 1
-        mm = g.tensor.matmul_mx(T.zp[:, 512 * i:512 * i + NC], T.w1c[:, NC * k:NC * k + NC], T.w1s[:, NC * k:NC * k + NC],
-                                T.xc[:, NC * j:NC * j + NC], T.xs[:, NC * j:NC * j + NC], done[i] == 1, done[i] == N)
-        if done[i] == N:
-            mm.then_inc(S["z%d" % i], 1)
+            g.tensor.wait_ge(S["arr%d" % j], 2 * _count(topo.mask(_sender(T, topo, j, kind[(j, r)]), core)))
+        for i in (0, 1):
+            k = N * i + j
+            g.tensor.wait_ge(S["wq%d" % k], 1)
+            mm = g.tensor.matmul_mx(T.zp[:, 512 * i:512 * i + NC], T.w1c[:, NC * k:NC * k + NC],
+                                    T.w1s[:, NC * k:NC * k + NC], T.xc[:, NC * j:NC * j + NC],
+                                    T.xs[:, NC * j:NC * j + NC], n_done == 0, n_done == N - 1)
+            if n_done == N - 1:
+                mm.then_inc(S["z%d" % i], 1)
     g.tensor.wait_ge(S.hq, 1)
     g.tensor.wait_ge(S.w2q, 1)
     g.tensor.matmul_mx(T.zp[:, 1024:1024 + NC], T.w2c[:, 0:NC], T.w2s[:, 0:NC], T.hc[:, 0:NC], T.hs[:, 0:NC], True, False)
@@ -157,11 +264,9 @@ def rank_program(g, core, T, topo):
     g.tensor.matmul_mx(T.zp[:, 1024:1024 + NC], T.w2c[:, NC:2 * NC], T.w2s[:, NC:2 * NC], T.hc[:, NC:2 * NC],
                        T.hs[:, NC:2 * NC], False, True).then_inc(S.ymm, 1)
 
-    for i in (0, 1):
-        g.scalar.wait_ge(S["z%d" % i], 1)
-        for b, sc in ((2 * i, C), (2 * i + 1, -C)):
-            g.scalar.activation(T.ht[:, b:TW:4], T.zp[:, 512 * i:512 * i + NC], ActivationFunctionType.Relu,
-                                scale=sc).then_inc(S.rdone, 1)
+    g.scalar.wait_ge(S.z0, 1)
+    for b, sc in ((0, C), (1, -C)):
+        g.scalar.activation(T.ht[:, b:TW:4], T.zp[:, 0:NC], ActivationFunctionType.Relu, scale=sc).then_inc(S.rdone, 1)
     g.scalar.wait_ge(S.rdone, 4)
     g.scalar.wait_ge(S.hgate, 1)
     g.scalar.dma_start(T.h[:], T.ht[:]).then_inc(S.hst, 16)

from concourse.bass import DstId, RemoteDMATransfer
from concourse.mybir import dt, AluOpType, ActivationFunctionType

N = 7
NC = 128
TW = 512
C = 0.00869
PRE = 4
FIRST = {1: [1], 2: [2], 3: [3], 4: [4], 5: [5], 6: [4, 2]}
LAST = {1: [1], 2: [1, 1], 3: [2, 1], 4: [3, 1], 5: [4, 1], 6: [4, 2], 7: [4, 2, 1]}
MAXCH = 5

SCRATCH = {
    "xt": ("sbuf", [128, TW], "bfloat16"),
    "w1t": ("sbuf", [128, 2 * N * TW], "bfloat16"),
    "w2t": ("sbuf", [128, 2 * TW], "bfloat16"),
    "ht": ("sbuf", [128, TW], "bfloat16"),
    "yt": ("sbuf", [128, NC], "float32"),
    "xc": ("sbuf", [128, N * NC], "float8_e4m3fn_x4"),
    "xs": ("sbuf", [128, N * NC], "uint8"),
    "w1c": ("sbuf", [128, 2 * N * NC], "float8_e4m3fn_x4"),
    "w1s": ("sbuf", [128, 2 * N * NC], "uint8"),
    "w2c": ("sbuf", [128, 2 * NC], "float8_e4m3fn_x4"),
    "w2s": ("sbuf", [128, 2 * NC], "uint8"),
    "hc": ("sbuf", [128, 2 * NC], "float8_e4m3fn_x4"),
    "hs": ("sbuf", [128, 2 * NC], "uint8"),
    "zp": ("psum", [128, 3 * 512], "float32"),
}
SEMAPHORES = (["lx", "lsec", "xq", "xsent", "gate", "z0", "z1", "rdone", "hq", "hsent", "hgate", "w2q", "harr", "ymm",
               "ycp", "yst", "hst", "pin", "cin", "fsent"]
              + ["lw%d" % i for i in range(MAXCH)] + ["wq%d" % k for k in range(2 * N)] + ["arr%d" % j for j in range(N)])

KINDS = [(True, 0), (False, 0), (True, 1), (False, 1), (True, 2), (False, 2)]
_CACHE = {}


def _count(mask):
    return bin(mask).count("1")


def _helpers(rc, T, topo):
    others = [d for d in T.cores if d != rc]
    cand = [c for c in range(topo.CORES_PER_CHIP * topo.CHIPS)
            if topo.chip(c) == topo.chip(rc) and c not in T.cores and all(topo.may_write(c, d) for d in others)]
    near = [c for c in cand if topo.die(c) == topo.die(rc)]
    far = [c for c in cand if topo.die(c) != topo.die(rc)]
    return near[0], far[0], far[1]


def _route(a, b, topo):
    if a == b:
        return []
    if topo.same_plane(a, b):
        return [("out", a), ("in", b)]
    if topo.mates(a, b):
        return [("mate", a)]
    m = [c for c in range(topo.CHIPS) if topo.mates(a, c)][0]
    return [("mate", a), ("out", m), ("in", b)]


def _subsets(items, k):
    if k == 0:
        return [[]]
    return [[items[i]] + rest for i in range(len(items)) for rest in _subsets(items[i + 1:], k - 1)]


def _match(edges, n):
    owner = {}

    def aug(s, seen):
        for d in range(n):
            if (s, d) in edges and d not in seen:
                seen.add(d)
                if d not in owner or aug(owner[d], seen):
                    owner[d] = s
                    return True
        return False

    for s in range(n):
        aug(s, set())
    return {s: d for d, s in owner.items()}


def _plan(T, topo):
    if "plan" in _CACHE:
        return _CACHE["plan"]
    n = len(T.cores)
    ch = [topo.chip(c) for c in T.cores]
    total = {}
    for s in range(n):
        for d in range(n):
            for l in _route(ch[s], ch[d], topo):
                total[l] = total.get(l, 0) + 1
    half = (n - 1) // 2
    res = []

    def rec(s, load, got):
        if s == n:
            return True
        others = [d for d in range(n) if d != s]
        for near in _subsets(others, half):
            l2, g2, ok = dict(load), dict(got), True
            for d in others:
                side = d in near
                g2[(d, side)] = g2.get((d, side), 0) + 1
                ok = ok and g2[(d, side)] <= half
                for l in _route(ch[s], ch[d], topo):
                    l2[(l, side)] = l2.get((l, side), 0) + 1
                    ok = ok and l2[(l, side)] <= (total[l] + 1) // 2
            if ok:
                res.append(near)
                if rec(s + 1, l2, g2):
                    return True
                res.pop()
        return False

    rec(0, {}, {})
    kind = {}
    for side in (True, False):
        edges = {(s, d) for s in range(n) for d in range(n) if d != s and (d in res[s]) == side}
        for k in range(half):
            for s, d in _match(edges, n).items():
                kind[(s, d)] = (side, k)
                edges.discard((s, d))
    _CACHE["plan"] = kind
    return kind


def _dest(kind, s, k):
    return [d for d in range(N) if kind.get((s, d)) == k][0]


def _sender(T, topo, s, k):
    near, far2, far1 = _helpers(T.cores[s], T, topo)
    if k[0]:
        return T.cores[s] if k[1] == 0 else near
    return far1 if k[1] == 0 else far2


def _multi(src_core, dsts, topo, src, dst, sem):
    mask = topo.mask(src_core, dsts[0])
    for d in dsts:
        mask &= topo.mask(src_core, d)
    ids = [DstId(rid=topo.addr(d)[0], pnc=topo.addr(d)[1]) for d in dsts]
    return RemoteDMATransfer(dst_ids=ids, dma_engine_mask=mask, remote_sem=sem, srcs=[src], dsts=[dst for _ in dsts]), _count(mask)


def _pieces(r):
    out = [(0, PRE), (PRE, N)]
    runs = [(N, 2 * N)] if r == 0 else [(N + r, 2 * N), (N, N + r)]
    for i, (a, b) in enumerate(runs):
        for n in (LAST if i == len(runs) - 1 else FIRST)[b - a]:
            out.append((a, a + n))
            a += n
    return out


def _pass_on(g, core, T, topo, s, dsts, sem_sent):
    sl = slice(NC * s, NC * s + NC)
    sent = 0
    for d in dsts:
        rid, pid, _ = topo.addr(d)
        m = topo.mask(core, d)
        g.remote_dma(T.xc[:, sl].bitcast(dt.uint8), T.xc[:, sl].bitcast(dt.uint8), T.sem["arr%d" % s], sem_sent, pid, rid, m)
        sent += _count(m)
    return sent


def _helper_program(g, core, T, topo, s, dsts):
    sl = slice(NC * s, NC * s + NC)
    n_in = _count(topo.mask(T.cores[s], core))
    g.wait_ge(T.sem.pin, n_in)
    t, sent = _multi(core, dsts, topo, T.xs[:, sl], T.xs[:, sl], T.sem["arr%d" % s])
    g.remote_dma_fused([t], local_sem=T.sem.fsent)
    g.wait_ge(T.sem.cin, n_in)
    sent += _pass_on(g, core, T, topo, s, dsts, T.sem.fsent)
    g.wait_ge(T.sem.fsent, sent)


def rank_program(g, core, T, topo):
    r = T.rank_of(core)
    kind = _plan(T, topo)
    if r is None:
        for s, rc in enumerate(T.cores):
            near, far2, far1 = _helpers(rc, T, topo)
            for h, ks in ((near, [(True, 1), (True, 2)]), (far2, [(False, 1), (False, 2)]), (far1, [(False, 0)])):
                if core == h:
                    _helper_program(g, core, T, topo, s, [T.cores[_dest(kind, s, k)] for k in ks])
        return

    S = T.sem
    own = slice(NC * r, NC * r + NC)
    pieces = _pieces(r)

    g.sync.dma_start(T.xt[:], T.x[:]).then_inc(S.lx, 16)
    for i, (a, b) in enumerate(pieces):
        if i == 1:
            g.sync.wait_ge(S.gate, 1)
            g.sync.dma_start(T.w2t[:], T.w2[:]).then_inc(S.lsec, 16)
        g.sync.dma_start(T.w1t[:, TW * a:TW * b], T.w1[:, TW * a:TW * b]).then_inc(S["lw%d" % i], 16)
    g.sync.wait_ge(S.ycp, 1)
    g.sync.dma_start(T.y[:], T.yt[:]).then_inc(S.yst, 16)
    g.sync.wait_ge(S.yst, 16)

    g.vector.wait_ge(S.lx, 16)
    g.vector.quantize_mx(T.xc[:, own], T.xs[:, own], T.xt[:]).then_inc(S.xq, 1)
    for i, (a, b) in enumerate(pieces):
        if i == 1:
            g.vector.wait_ge(S.lsec, 16)
            g.vector.quantize_mx(T.w2c[:], T.w2s[:], T.w2t[:]).then_inc(S.w2q, 1)
        g.vector.wait_ge(S["lw%d" % i], 16)
        for k in range(a, b):
            g.vector.quantize_mx(T.w1c[:, NC * k:NC * k + NC], T.w1s[:, NC * k:NC * k + NC],
                                 T.w1t[:, TW * k:TW * k + TW]).then_inc(S["wq%d" % k], 1)
    g.vector.wait_ge(S.z1, 1)
    for b, sc in ((2, C), (3, -C)):
        g.vector.tensor_scalar(T.ht[:, b:TW:4], T.zp[:, 512:512 + NC], sc, 0.0, AluOpType.mult,
                               AluOpType.max).then_inc(S.rdone, 1)
    g.vector.wait_ge(S.rdone, 4)
    g.vector.quantize_mx(T.hc[:, 0:NC], T.hs[:, 0:NC], T.ht[:]).then_inc(S.hq, 1)
    g.vector.wait_ge(S.ymm, 1)
    g.vector.tensor_copy(T.yt[:], T.zp[:, 1024:1024 + NC]).then_inc(S.ycp, 1)

    helpers = list(_helpers(core, T, topo))
    g.wait_ge(S.xq, 1)
    tp, n_on = _multi(core, helpers, topo, T.xs[:, own], T.xs[:, own], S.pin)
    g.remote_dma_fused([tp], local_sem=S.xsent)
    tc, _ = _multi(core, helpers, topo, T.xc[:, own].bitcast(dt.uint8), T.xc[:, own].bitcast(dt.uint8), S.cin)
    g.remote_dma_fused([tc], local_sem=S.xsent)
    straight = [T.cores[_dest(kind, r, (True, 0))]]
    td, n_off = _multi(core, straight, topo, T.xs[:, own], T.xs[:, own], S["arr%d" % r])
    g.remote_dma_fused([td], local_sem=S.xsent)
    n_off += _pass_on(g, core, T, topo, r, straight, S.xsent)
    g.sem_inc(S.gate, 1)
    prev = T.cores[(r - 1) % N]
    rid, pid, _ = topo.addr(prev)
    hm = topo.mask(core, prev)
    g.wait_ge(S.hq, 1)
    g.remote_dma(T.hc[:, NC:2 * NC].bitcast(dt.uint8), T.hc[:, 0:NC].bitcast(dt.uint8), S.harr, S.hsent, pid, rid, hm)
    g.remote_dma(T.hs[:, NC:2 * NC], T.hs[:, 0:NC], S.harr, S.hsent, pid, rid, hm)
    g.sem_inc(S.hgate, 1)
    g.wait_ge(S.xsent, 2 * n_on + n_off)
    g.wait_ge(S.hsent, 2 * _count(hm))

    order = [r] + sorted([j for j in range(N) if j != r], key=lambda j: KINDS.index(kind[(j, r)]))
    for n_done, j in enumerate(order):
        if j == r:
            g.tensor.wait_ge(S.xq, 1)
        else:
            g.tensor.wait_ge(S["arr%d" % j], 2 * _count(topo.mask(_sender(T, topo, j, kind[(j, r)]), core)))
        for i in (0, 1):
            k = N * i + j
            g.tensor.wait_ge(S["wq%d" % k], 1)
            mm = g.tensor.matmul_mx(T.zp[:, 512 * i:512 * i + NC], T.w1c[:, NC * k:NC * k + NC],
                                    T.w1s[:, NC * k:NC * k + NC], T.xc[:, NC * j:NC * j + NC],
                                    T.xs[:, NC * j:NC * j + NC], n_done == 0, n_done == N - 1)
            if n_done == N - 1:
                mm.then_inc(S["z%d" % i], 1)
    g.tensor.wait_ge(S.hq, 1)
    g.tensor.wait_ge(S.w2q, 1)
    g.tensor.matmul_mx(T.zp[:, 1024:1024 + NC], T.w2c[:, 0:NC], T.w2s[:, 0:NC], T.hc[:, 0:NC], T.hs[:, 0:NC], True, False)
    nxt = T.cores[(r + 1) % N]
    g.tensor.wait_ge(S.harr, 2 * _count(topo.mask(nxt, core)))
    g.tensor.matmul_mx(T.zp[:, 1024:1024 + NC], T.w2c[:, NC:2 * NC], T.w2s[:, NC:2 * NC], T.hc[:, NC:2 * NC],
                       T.hs[:, NC:2 * NC], False, True).then_inc(S.ymm, 1)

    g.scalar.wait_ge(S.z0, 1)
    for b, sc in ((0, C), (1, -C)):
        g.scalar.activation(T.ht[:, b:TW:4], T.zp[:, 0:NC], ActivationFunctionType.Relu, scale=sc).then_inc(S.rdone, 1)
    g.scalar.wait_ge(S.rdone, 4)
    g.scalar.wait_ge(S.hgate, 1)
    g.scalar.dma_start(T.h[:], T.ht[:]).then_inc(S.hst, 16)
    g.scalar.wait_ge(S.hst, 16)
